import numpy as np
import ml_dtypes


def mxq(x, axis, fmt="e4m3"):
    dtype, down = {"e4m3": (ml_dtypes.float8_e4m3fn, 7), "e5m2": (ml_dtypes.float8_e5m2, 14)}[fmt]
    v = np.moveaxis(np.asarray(x, np.float32).astype(ml_dtypes.bfloat16).astype(np.float64), axis, -1)
    blocks = v.reshape(v.shape[:-1] + (-1, 32))
    amax = np.abs(blocks).max(-1, keepdims=True)
    byte = np.maximum(np.where(amax > 0, np.frexp(amax)[1] - 1 + 127, 0) - down, 1)
    scale = np.exp2(byte - 127.0)
    codes = (blocks / scale).astype(np.float32).astype(dtype).astype(np.float64)
    return np.moveaxis((codes * scale).reshape(v.shape), -1, axis)


WIDE = False


def mx_kscale(k):
    if not WIDE:
        return np.ones(k)
    levels = np.array([30, -30])
    if k % 512:
        return np.exp2(np.random.permutation(np.resize(levels, k // 32))).repeat(32)
    a = np.empty((k // 512, 16))
    for p in range(k // 512):
        a[p, :8] = np.random.permutation(np.resize(levels, 8))
        for g in range(8):
            far = levels[np.abs(levels - a[p, g]) >= 10]
            a[p, g + 8] = far[np.random.randint(len(far))]
    return np.exp2(a.ravel()).repeat(32)


BF16 = ml_dtypes.bfloat16


def bf(x):
    return np.asarray(x, np.float32).astype(BF16)


def f64(x):
    return np.asarray(x).astype(np.float64)


E2M1 = np.array([0.0, 0.5, 1.0, 1.5, 2.0, 3.0, 4.0, 6.0, -0.0, -0.5, -1.0, -1.5, -2.0, -3.0, -4.0, -6.0])


def pack_weight(w, fmt):
    k, n = w.shape
    w = f64(bf(w)).reshape(k // 32, 32, n)
    amax = np.abs(w).max(1)
    if fmt in ("e4m3", "e5m2"):
        byte = np.frexp(amax)[1] - 1 + 127 - (7 if fmt == "e4m3" else 14)
    else:
        mant, ex = np.frexp(amax / 6.0)
        byte = np.where(mant > 0.5, ex, ex - 1) + 127
    byte = np.clip(np.where(amax > 0, byte, 1), 1, 254)
    scaled = (w * np.exp2(127.0 - byte)[:, None, :]).reshape(k, n).astype(np.float32)
    by_word = np.ascontiguousarray(scaled.reshape(k // 512, 128, 4, n).transpose(0, 1, 3, 2))
    if fmt in ("e4m3", "e5m2"):
        words = by_word.astype(ml_dtypes.float8_e4m3fn if fmt == "e4m3" else ml_dtypes.float8_e5m2).view(np.uint8)
    else:
        c = by_word.astype(ml_dtypes.float4_e2m1fn).view(np.uint8) & 0xF
        words = c[..., 0::2] | (c[..., 1::2] << 4)
    return np.ascontiguousarray(words), np.ascontiguousarray(byte.astype(np.uint8).reshape(k // 512, 16, n))


def unpack_weight(words, scales, fmt):
    g, p, n, _ = words.shape
    if fmt in ("e4m3", "e5m2"):
        vals = np.ascontiguousarray(words).view(ml_dtypes.float8_e4m3fn if fmt == "e4m3" else ml_dtypes.float8_e5m2).astype(np.float64)
    else:
        nib = np.empty((g, p, n, 4), np.uint8)
        nib[..., 0::2] = words & 0xF
        nib[..., 1::2] = words >> 4
        vals = E2M1[nib]
    vals = vals * np.repeat(np.exp2(scales.astype(np.float64) - 127.0), 8, axis=1)[..., None]
    return vals.transpose(0, 1, 3, 2).reshape(g * 512, n)


K, M, N = 3072, 1536, 1024


def setup_inputs():
    s = mx_kscale(K)
    err = np.random.standard_normal((K, N)) * np.exp(0.5 * np.random.standard_normal((K, N)))
    e_words, e_scales = pack_weight(err / s[:, None], "e5m2")
    return {"e_words": e_words,
            "e_scales": e_scales,
            "gain": bf(np.random.standard_normal((K, M)) / np.sqrt(K) * s[:, None]),
            "u": bf(np.random.standard_normal((M, N))),
            "keep": bf(np.random.uniform(0.8, 0.95, (M,))),
            "rate": bf(1 + 0.1 * np.random.standard_normal((N,)))}


def reference(e_words, e_scales, gain, u, keep, rate):
    err = unpack_weight(e_words, e_scales, "e5m2")
    gq = mxq(f64(gain), 0, "e4m3")
    step = gq.T @ err
    kept = f64(keep)[:, None] * f64(u)
    u_next = kept + f64(rate)[None, :] * step
    return u_next

@@ -1,0 +1,276 @@
+from contextlib import ExitStack
+
+import concourse.mybir as mybir
+from concourse.masks import make_identity
+
+K, M, N = 3072, 1536, 1024
+FLOPS = 2 * K * M * N
+
+F32 = mybir.dt.float32
+BF16 = mybir.dt.bfloat16
+I32 = mybir.dt.int32
+U32 = mybir.dt.uint32
+U8 = mybir.dt.uint8
+E4M3X4 = mybir.dt.float8_e4m3fn_x4
+E5M2X4 = mybir.dt.float8_e5m2_x4
+MULT = mybir.AluOpType.mult
+ADD = mybir.AluOpType.add
+
+P = 128
+PACK = 4
+PASSES = K // (P * PACK)
+TILES = M // P
+HALF = 512
+BANKS = 8
+GROUP_BUFS = 5
+RAW_BLOCK = 4
+
+def plan_with(gs=3, early=0, uat=(2,6,12,14,18,18), lag=2, pre=4, vhelp=(), rate=2, scsplit=2, qfirst=1, b2split=False, fine=2, vfirst=2, scat=1):
+    sync=[]; tail=[]
+    rest=[('gain',g,4,2) for g in range(6)]+[('gain',g,6,2) for g in range(6)]
+    rest+= [('gain',g,j,2) for j in (8,10) for g in range(6)] if b2split else [('gain',g,8,4) for g in range(6)]
+    for g in range(6):
+        sync.append(('gain',g,0,4))
+        if g<gs: sync.append(('err',g,(0,1)))
+        else: sync.append(('err',g,(0,))); tail.append(('err',g,(1,)))
+        if g==0: sync.append(('scales',tuple(range(scsplit))))
+        if g==scat: sync.append(('scales',tuple(range(scsplit,6))))
+    k=0
+    for t in tail:
+        sync.append(t)
+        if k<early: sync.append(rest[k]); k+=1
+    for i in range(k,len(rest)+1):
+        for kk,p in enumerate(uat):
+            if max(k,min(p,len(rest)))==i: sync.append(('u',2*kk,2))
+        if i<len(rest): sync.append(rest[i])
+    for j in range(10): sync.append(('store',j,1,(0,1)))
+    for j in (10,11): sync+= [('store',j,1,(0,)),('store',j,1,(1,))]
+    act=[];dve=[];pe=[]
+    for g in range(6):
+        dve+=[('inter',g,0,vfirst)]; act+=[('inter',g,vfirst,4-vfirst)]
+        dve+=[('quant',g,0,vfirst),('quant',g,vfirst,4-vfirst)]
+        pe+=[('mm',j,h,g) for j in range(4) for h in range(2) if g<gs or h==0]
+    pe+=[('mm',j,1,g) for g in range(gs,6) for j in range(4)]
+    steps=[(j,2,g) for j in range(4,12-fine,2) for g in range(6)]+[(j,1,g) for j in range(12-fine,12) for g in range(6)]
+    first=[('op1',j,0) for j in range(4)]
+    pend=first+[('op2',0,0),('op2',1,0),('op1',0,1),('op1',1,1),('op2',0,1),('op2',1,1),('op2',2,0),('op2',3,0),('op1',2,1),('op1',3,1),('op2',2,1),('op2',3,1)]
+    for unused in range(pre): dve.append(pend.pop(0))
+    later=[]; credit=0
+    for i,(j,n,g) in enumerate(steps):
+        if i in vhelp: dve.append(('inter',g,j,n))
+        else: act.append(('inter',g,j,n))
+        if i in vhelp and pend: dve.append(pend.pop(0)); credit-=1
+        dve.append(('quant',g,j,n))
+        pe+=[('mm',jj,h,g) for jj in range(j,j+n) for h in range(2)]
+        for (due,ops) in list(later):
+            if due<=i: pend+=ops; later.remove((due,ops))
+        credit+=rate*n/2
+        while credit>=1 and pend: dve.append(pend.pop(0)); credit-=1
+        if not pend: credit=0
+        if g==5:
+            ops=[]
+            for jj in range(j,j+n): ops+=[('op1',jj,0),('op1',jj,1),('op2',jj,0),('op2',jj,1)]
+            later.append((i+(lag if n==2 else lag+1),ops))
+    for due,ops in later: pend+=ops
+    dve+=pend
+    return dict(sync=sync,act=act,dve=dve,pe=pe)
+
+
+def plan():
+    queues = plan_with(gs=3, early=2, pre=4, lag=2, rate=2, fine=4)
+    queues["dve"].insert(4, ("consts",))
+    return queues
+
+
+def covers(step):
+    kind = step[0]
+    if kind in ("gain", "inter", "quant"):
+        return [(kind, step[1], j) for j in range(step[2], step[2] + step[3])]
+    if kind == "err":
+        return [(kind, step[1], h) for h in step[2]]
+    if kind == "scales":
+        return [(kind, g) for g in step[1]]
+    if kind == "u":
+        return [(kind, j) for j in range(step[1], step[1] + step[2])]
+    return [step]
+
+
+def needs(step, units):
+    kind = step[0]
+    if kind == "gain":
+        return [("inter", step[1], j) for j in range(RAW_BLOCK) if step[2] >= 2 * RAW_BLOCK]
+    if kind == "inter":
+        return [("gain", step[1], j) for j in range(step[2], step[2] + step[3])]
+    if kind == "quant":
+        return [("inter", step[1], j) for j in range(step[2], step[2] + step[3])]
+    if kind == "mm":
+        j, h, g = step[1:]
+        keys = [("quant", g, j), ("err", g, h), ("scales", g)]
+        place = units.index((j, h))
+        if g == 0 and place >= BANKS:
+            keys.append(("op1",) + units[place - BANKS])
+        if g == 0 and place in (6, 7):
+            keys.append(("consts",))
+        return keys
+    if kind == "op1":
+        return [("mm", step[1], step[2], PASSES - 1), ("consts",)]
+    if kind == "op2":
+        return [("op1", step[1], step[2]), ("u", step[1])]
+    if kind == "store":
+        return [("op2", j, h) for j in range(step[1], step[1] + step[2]) for h in step[3]]
+    return []
+
+
+def merge(queues):
+    units = [(s[1], s[2]) for s in queues["pe"] if s[3] == 0]
+    made = set()
+    place = {engine: 0 for engine in queues}
+    waiting = {"act": [], "dve": []}
+    order = []
+    total = sum(len(q) for q in queues.values())
+    while len(order) < total:
+        before = len(order)
+        for engine, queue in queues.items():
+            if place[engine] == len(queue):
+                continue
+            step = queue[place[engine]]
+            if not all(key in made for key in needs(step, units)):
+                continue
+            if step[0] == "inter":
+                ring = waiting[engine]
+                if len(ring) >= GROUP_BUFS and ("quant", ring[-GROUP_BUFS][1], ring[-GROUP_BUFS][2]) not in made:
+                    continue
+                ring.append(step)
+            for key in covers(step):
+                made.add(key)
+            order.append((engine, step))
+            place[engine] += 1
+        assert len(order) > before
+    return order
+
+
+def tile_leaky_iterative_learning_update_e2_kernel(tc, e_words, e_scales, gain, u, keep, rate, out):
+    nc = tc.nc
+    queues = plan()
+
+    with ExitStack() as ctx:
+        hold = ctx.enter_context(tc.tile_pool(name="hold", bufs=1))
+        stage = ctx.enter_context(tc.tile_pool(name="stage", bufs=GROUP_BUFS))
+        psum = ctx.enter_context(tc.psum_pool(name="psum", bufs=1))
+        ctx.enter_context(tc.manual_schedule())
+
+        err_words = hold.tile([P, PASSES, N], U32, align_bytes=64)
+        err_scales = hold.tile([P, PASSES, N], U8, align_bytes=64)
+        gain_words = hold.tile([P, PASSES, M], U32, align_bytes=64)
+        gain_scales = hold.tile([P, PASSES, M], U8, align_bytes=64)
+        raw = hold.tile([P, 2, PASSES, PACK * RAW_BLOCK * P], BF16, align_bytes=64)
+        u_sb = hold.tile([P, TILES, N], BF16)
+        res = hold.tile([P, TILES, N], F32)
+        ident = hold.tile([P, P], BF16)
+        keep_rows = hold.tile([P, P], BF16)
+        rate_cols = hold.tile([P, N // P], BF16)
+        keep_cols = hold.tile([P, TILES], F32)
+        rate_all = hold.tile([P, N], BF16)
+
+        u_tiles = u.rearrange("(j p) n -> p j n", p=P)
+        out_tiles = out.rearrange("(j p) n -> p j n", p=P)
+
+        nc.vector.memset(keep_rows[:], 0.0)
+        nc.scalar.dma_start(out=rate_cols[:], in_=rate.rearrange("(p i) -> p i", p=P))
+        nc.scalar.dma_start(out=keep_rows[0:TILES, :], in_=keep.rearrange("(j p) -> j p", p=P))
+        make_identity(nc, ident[:])
+        for step in queues["sync"]:
+            if step[0] == "scales":
+                nc.vector.memset(err_scales[:, step[1][0] : step[1][-1] + 1, :].bitcast(I32), 0)
+        rate_ps = psum.tile([P, N // P, P], BF16, tag="bank6", name="rate_ps")
+        for i in range(N // P):
+            nc.tensor.transpose(rate_ps[:, i, :], rate_cols[:, i : i + 1].to_broadcast([P, P]), ident[:])
+        keep_ps = psum.tile([P, P], BF16, tag="bank7", name="keep_ps")
+        nc.tensor.transpose(keep_ps[:], keep_rows[:], ident[:])
+
+        raw_view = {}
+        grouped = {}
+        bank = {}
+
+        def raw_of(g, j0, nj, load):
+            slot = raw[:, (load[2] // RAW_BLOCK) % 2, g, :]
+            first = (load[2] % RAW_BLOCK) * P * PACK
+            rows = slot[:, first : first + load[3] * P * PACK].rearrange("p (t w) -> p t w", t=PACK)
+            return rows[:, :, (j0 - load[2]) * P : (j0 - load[2] + nj) * P]
+
+        def emit(engine, step):
+            kind = step[0]
+            if kind == "gain":
+                g, j0, nj = step[1:]
+                for j in range(j0, j0 + nj):
+                    raw_view[(j, g)] = step
+                rows = gain[g * P * PACK : (g + 1) * P * PACK, j0 * P : (j0 + nj) * P]
+                nc.sync.dma_start(out=raw_of(g, j0, nj, step), in_=rows.rearrange("(p t) w -> p t w", t=PACK))
+            elif kind == "err":
+                g, halves = step[1:]
+                lo, hi = halves[0] * HALF, (halves[-1] + 1) * HALF
+                src = e_words[g].rearrange("p n t -> p (n t)")[:, lo * PACK : hi * PACK].bitcast(I32)
+                nc.sync.dma_start(out=err_words[:, g, lo:hi].bitcast(I32), in_=src)
+            elif kind == "scales":
+                g0, g1 = step[1][0], step[1][-1] + 1
+                for r in range(4):
+                    src = e_scales[g0:g1, r:16:4, :].rearrange("g q n -> q g n").bitcast(I32)
+                    nc.sync.dma_start(out=err_scales[r:P:32, g0:g1, :].bitcast(I32), in_=src)
+            elif kind == "u":
+                j0, nj = step[1:]
+                nc.sync.dma_start(out=u_sb[:, j0 : j0 + nj, :], in_=u_tiles[:, j0 : j0 + nj, :])
+            elif kind == "store":
+                j0, nj, halves = step[1:]
+                cols = slice(halves[0] * HALF, (halves[-1] + 1) * HALF)
+                nc.sync.dma_start(out=out_tiles[:, j0 : j0 + nj, cols], in_=res[:, j0 : j0 + nj, cols])
+            elif kind == "consts":
+                nc.vector.tensor_copy(out=rate_all[:].rearrange("p (n i) -> p n i", i=N // P), in_=rate_ps[:].rearrange("p i n -> p n i"))
+                nc.vector.tensor_copy(out=keep_cols[:], in_=keep_ps[:, 0:TILES])
+            elif kind == "inter":
+                g, j0, nj = step[1:]
+                side = stage.tile([P, nj * P, PACK], BF16, align_bytes=64, tag="side_" + engine, name="side")
+                grouped[(g, j0)] = side
+                src = raw_of(g, j0, nj, raw_view[(j0, g)])
+                dst = side[:]
+                src = src.rearrange("p t (c i) -> p c t i", i=4)
+                dst = dst.rearrange("p (c i) t -> p c t i", i=4)
+                if engine == "act":
+                    nc.scalar.copy(out=dst, in_=src)
+                else:
+                    nc.vector.tensor_copy(out=dst, in_=src)
+            elif kind == "quant":
+                g, j0, nj = step[1:]
+                cols = slice(j0 * P, (j0 + nj) * P)
+                nc.vector.quantize_mx(
+                    out=gain_words[:, g, cols].bitcast(E4M3X4),
+                    scales=gain_scales[:, g, cols],
+                    in_=grouped[(g, j0)][:].rearrange("p w t -> p (w t)"),
+                )
+            elif kind == "mm":
+                j, h, g = step[1:]
+                if g == 0:
+                    bank[(j, h)] = psum.tile([P, HALF], F32, tag="bank%d" % (len(bank) % BANKS), name="acc")
+                m_cols = slice(j * P, (j + 1) * P)
+                n_cols = slice(h * HALF, (h + 1) * HALF)
+                nc.tensor.matmul_mx(
+                    out=bank[(j, h)][:],
+                    lhsT=gain_words[:, g, m_cols].bitcast(E4M3X4),
+                    lhsT_scale=gain_scales[:, g, m_cols],
+                    rhs=err_words[:, g, n_cols].bitcast(E5M2X4),
+                    rhs_scale=err_scales[:, g, n_cols],
+                    start=(g == 0),
+                    stop=(g == PASSES - 1),
+                )
+            elif kind == "op1":
+                j, h = step[1:]
+                cols = slice(h * HALF, (h + 1) * HALF)
+                nc.vector.tensor_tensor(out=res[:, j, cols], in0=bank[(j, h)][:], in1=rate_all[:, cols], op=MULT)
+            else:
+                j, h = step[1:]
+                cols = slice(h * HALF, (h + 1) * HALF)
+                nc.vector.scalar_tensor_tensor(
+                    out=res[:, j, cols], in0=u_sb[:, j, cols], scalar=keep_cols[:, j : j + 1], in1=res[:, j, cols], op0=MULT, op1=ADD
+                )
+
+        for engine, step in merge(queues):
+            emit(engine, step)

@@ -22,63 +22,88 @@ PASSES = K // (P * PACK)
 TILES = M // P
 HALF = 512
 BANKS = 8
-GROUP_BUFS = 5
-RAW_BLOCK = 4
+GROUP_BUFS = 6
+RAW_TILES = 9
+FIRST_TILES = 6
 
-def plan_with(gs=3, early=0, uat=(2,6,12,14,18,18), lag=2, pre=4, vhelp=(), rate=2, scsplit=2, qfirst=1, b2split=False, fine=2, vfirst=2, scat=1):
-    sync=[]; tail=[]
-    rest=[('gain',g,4,2) for g in range(6)]+[('gain',g,6,2) for g in range(6)]
-    rest+= [('gain',g,j,2) for j in (8,10) for g in range(6)] if b2split else [('gain',g,8,4) for g in range(6)]
+def plan_with(w0=6, gs=0, blocks=((6,2),(8,4)), groups=((6,2),(8,1),(9,1),(10,1),(11,1)), uat=(3,8,12,16,20,24), mix=6, lag=2, pre=4, rate=2, vhelp=(), split=((0,2,1),(2,1,1),(3,1,0),(4,2,0)), fill=0, qa=0, seq=1, big=0, usz=2, eup=0, cut=0, n1=6):
+    lead=8-w0
+    sync=[]
+    tail=[]
     for g in range(6):
-        sync.append(('gain',g,0,4))
+        if g>=6-cut: sync+=[('gain',g,0,2),('gain',g,2,w0-2)]
+        else: sync.append(('gain',g,0,w0))
         if g<gs: sync.append(('err',g,(0,1)))
-        else: sync.append(('err',g,(0,))); tail.append(('err',g,(1,)))
-        if g==0: sync.append(('scales',tuple(range(scsplit))))
-        if g==scat: sync.append(('scales',tuple(range(scsplit,6))))
-    k=0
-    for t in tail:
-        sync.append(t)
-        if k<early: sync.append(rest[k]); k+=1
-    for i in range(k,len(rest)+1):
-        for kk,p in enumerate(uat):
-            if max(k,min(p,len(rest)))==i: sync.append(('u',2*kk,2))
+        else:
+            sync.insert(len(sync)-(eup if g==5 else 0),('err',g,(0,)))
+            tail.append(('err',g,(1,)))
+    gains=[('gain',g,j,n) for (j,n) in blocks for g in range(6)]
+    rest=[]
+    while tail:
+        rest+=tail[:mix]
+        tail=tail[mix:]
+        if tail: rest.append(gains.pop(0))
+    rest+=gains
+    for i in range(len(rest)+1):
+        for kk,p in enumerate(uat[:12//usz]):
+            if min(p,len(rest))==i: sync.append(('u',usz*kk,usz))
         if i<len(rest): sync.append(rest[i])
-    for j in range(10): sync.append(('store',j,1,(0,1)))
-    for j in (10,11): sync+= [('store',j,1,(0,)),('store',j,1,(1,))]
-    act=[];dve=[];pe=[]
+    for j in range(0,2*big,2): sync.append(('store',j,2,(0,1)))
+    for j in range(2*big,11): sync.append(('store',j,1,(0,1)))
+    sync+= [('store',11,1,(0,)),('store',11,1,(1,))]
+    act=[]
+    dve=[]
+    pe=[]
     for g in range(6):
-        dve+=[('inter',g,0,vfirst)]; act+=[('inter',g,vfirst,4-vfirst)]
-        dve+=[('quant',g,0,vfirst),('quant',g,vfirst,4-vfirst)]
-        pe+=[('mm',j,h,g) for j in range(4) for h in range(2) if g<gs or h==0]
-    pe+=[('mm',j,1,g) for g in range(gs,6) for j in range(4)]
-    steps=[(j,2,g) for j in range(4,12-fine,2) for g in range(6)]+[(j,1,g) for j in range(12-fine,12) for g in range(6)]
-    first=[('op1',j,0) for j in range(4)]
-    pend=first+[('op2',0,0),('op2',1,0),('op1',0,1),('op1',1,1),('op2',0,1),('op2',1,1),('op2',2,0),('op2',3,0),('op1',2,1),('op1',3,1),('op2',2,1),('op2',3,1)]
+        mine=[(j,n) for (j,n,v) in split if v]
+        dve+=[('inter',g,j,n) for (j,n) in mine]
+        act+=[('inter',g,j,n) for (j,n,v) in split if not v]
+        dve+=[('quant',g,j,n) for (j,n,v) in split]
+        pe+=[('mm',j,0,g) for j in range(w0)]
+        if g<gs: pe+=[('mm',j,1,g) for j in range(lead)]
+    pe+=[('mm',j,1,g) for g in range(gs,6) for j in range(lead)]
+    pe+=[('mm',j,1,g) for j in range(lead,w0) for g in range(6)]
+    steps=[(j,n,g) for (j,n) in groups for g in range(6)]
+    for (j,n,g) in steps: pe+=[('mm',jj,h,g) for jj in range(j,j+n) for h in range(2) if jj<12-seq]
+    pe+=[('mm',j,h,g) for j in range(12-seq,12) for h in range(2) for g in range(6)]
+    for k in range(fill):
+        steps.insert(2*k+1,steps.pop(6+k))
+    pend=[('op1',j,0) for j in range(n1 if n1<w0 else w0)]
+    for j in range(w0):
+        if j>=n1: pend.append(('op1',j,0))
+        pend+=[('op1',j,1),('op2',j,0),('op2',j,1)] if j else [('op2',j,0),('op1',j,1),('op2',j,1)]
     for unused in range(pre): dve.append(pend.pop(0))
-    later=[]; credit=0
+    later=[]
+    credit=0
     for i,(j,n,g) in enumerate(steps):
         if i in vhelp: dve.append(('inter',g,j,n))
         else: act.append(('inter',g,j,n))
-        if i in vhelp and pend: dve.append(pend.pop(0)); credit-=1
+        if i in vhelp and pend:
+            dve.append(pend.pop(0))
+            credit-=1
         dve.append(('quant',g,j,n))
-        pe+=[('mm',jj,h,g) for jj in range(j,j+n) for h in range(2)]
         for (due,ops) in list(later):
-            if due<=i: pend+=ops; later.remove((due,ops))
-        credit+=rate*n/2
-        while credit>=1 and pend: dve.append(pend.pop(0)); credit-=1
+            if due<=i:
+                pend+=ops
+                later.remove((due,ops))
+        if i>=qa: credit+=rate*n/2
+        while credit>=1 and pend:
+            dve.append(pend.pop(0))
+            credit-=1
         if not pend: credit=0
         if g==5:
             ops=[]
             for jj in range(j,j+n): ops+=[('op1',jj,0),('op1',jj,1),('op2',jj,0),('op2',jj,1)]
-            later.append((i+(lag if n==2 else lag+1),ops))
+            if j+n==12: ops[-3:]=[ops[-2],ops[-3],ops[-1]]
+            later.append((i+lag,ops))
     for due,ops in later: pend+=ops
     dve+=pend
     return dict(sync=sync,act=act,dve=dve,pe=pe)
 
 
 def plan():
-    queues = plan_with(gs=3, early=2, pre=4, lag=2, rate=2, fine=4)
-    queues["dve"].insert(4, ("consts",))
+    queues = plan_with(**{'gs': 0, 'mix': 6, 'lag': 5, 'pre': 8, 'rate': 2, 'qa': 0, 'seq': 2, 'big': 2, 'n1': 6, 'groups': ((6, 1), (7, 1), (8, 1), (9, 1), (10, 1), (11, 1)), 'split': ((0, 1, 1), (1, 1, 0), (2, 2, 1), (4, 2, 0)), 'w0': 6, 'blocks': ((6,3),(9,3)), 'fill': 6, 'uat': (4,10,13,15,30,30)})
+    queues["dve"].insert(6, ("consts",))
     return queues
 
 
@@ -98,14 +123,14 @@ def covers(step):
 def needs(step, units):
     kind = step[0]
     if kind == "gain":
-        return [("inter", step[1], j) for j in range(RAW_BLOCK) if step[2] >= 2 * RAW_BLOCK]
+        return [("inter", step[1], j) for j in range(FIRST_TILES) if step[2] >= RAW_TILES]
     if kind == "inter":
         return [("gain", step[1], j) for j in range(step[2], step[2] + step[3])]
     if kind == "quant":
         return [("inter", step[1], j) for j in range(step[2], step[2] + step[3])]
     if kind == "mm":
         j, h, g = step[1:]
-        keys = [("quant", g, j), ("err", g, h), ("scales", g)]
+        keys = [("quant", g, j), ("err", g, h)]
         place = units.index((j, h))
         if g == 0 and place >= BANKS:
             keys.append(("op1",) + units[place - BANKS])
@@ -163,7 +188,7 @@ def tile_leaky_iterative_learning_update_e2_kernel(tc, e_words, e_scales, gain, 
         err_scales = hold.tile([P, PASSES, N], U8, align_bytes=64)
         gain_words = hold.tile([P, PASSES, M], U32, align_bytes=64)
         gain_scales = hold.tile([P, PASSES, M], U8, align_bytes=64)
-        raw = hold.tile([P, 2, PASSES, PACK * RAW_BLOCK * P], BF16, align_bytes=64)
+        raw = hold.tile([P, PASSES, PACK * RAW_TILES * P], BF16, align_bytes=64)
         u_sb = hold.tile([P, TILES, N], BF16)
         res = hold.tile([P, TILES, N], F32)
         ident = hold.tile([P, P], BF16)
@@ -175,13 +200,14 @@ def tile_leaky_iterative_learning_update_e2_kernel(tc, e_words, e_scales, gain, 
         u_tiles = u.rearrange("(j p) n -> p j n", p=P)
         out_tiles = out.rearrange("(j p) n -> p j n", p=P)
 
+        nc.vector.memset(err_scales[:].bitcast(I32), 0)
         nc.vector.memset(keep_rows[:], 0.0)
         nc.scalar.dma_start(out=rate_cols[:], in_=rate.rearrange("(p i) -> p i", p=P))
         nc.scalar.dma_start(out=keep_rows[0:TILES, :], in_=keep.rearrange("(j p) -> j p", p=P))
+        for r in range(4):
+            src = e_scales[:, r:16:4, :].rearrange("g q n -> q g n").bitcast(I32)
+            nc.gpsimd.dma_start(out=err_scales[r:P:32, :, :].bitcast(I32), in_=src)
         make_identity(nc, ident[:])
-        for step in queues["sync"]:
-            if step[0] == "scales":
-                nc.vector.memset(err_scales[:, step[1][0] : step[1][-1] + 1, :].bitcast(I32), 0)
         rate_ps = psum.tile([P, N // P, P], BF16, tag="bank6", name="rate_ps")
         for i in range(N // P):
             nc.tensor.transpose(rate_ps[:, i, :], rate_cols[:, i : i + 1].to_broadcast([P, P]), ident[:])
@@ -193,10 +219,14 @@ def tile_leaky_iterative_learning_update_e2_kernel(tc, e_words, e_scales, gain, 
         bank = {}
 
         def raw_of(g, j0, nj, load):
-            slot = raw[:, (load[2] // RAW_BLOCK) % 2, g, :]
-            first = (load[2] % RAW_BLOCK) * P * PACK
-            rows = slot[:, first : first + load[3] * P * PACK].rearrange("p (t w) -> p t w", t=PACK)
+            first = (load[2] % RAW_TILES) * P * PACK
+            rows = raw[:, g, first : first + load[3] * P * PACK].rearrange("p (t w) -> p t w", t=PACK)
             return rows[:, :, (j0 - load[2]) * P : (j0 - load[2] + nj) * P]
+
+        def parts_of(j, h):
+            count = 2 if (j, h) == (TILES - 1, 1) else 1
+            width = HALF // count
+            return [slice(h * HALF + c * width, h * HALF + (c + 1) * width) for c in range(count)]
 
         def emit(engine, step):
             kind = step[0]
@@ -211,18 +241,14 @@ def tile_leaky_iterative_learning_update_e2_kernel(tc, e_words, e_scales, gain, 
                 lo, hi = halves[0] * HALF, (halves[-1] + 1) * HALF
                 src = e_words[g].rearrange("p n t -> p (n t)")[:, lo * PACK : hi * PACK].bitcast(I32)
                 nc.sync.dma_start(out=err_words[:, g, lo:hi].bitcast(I32), in_=src)
-            elif kind == "scales":
-                g0, g1 = step[1][0], step[1][-1] + 1
-                for r in range(4):
-                    src = e_scales[g0:g1, r:16:4, :].rearrange("g q n -> q g n").bitcast(I32)
-                    nc.sync.dma_start(out=err_scales[r:P:32, g0:g1, :].bitcast(I32), in_=src)
             elif kind == "u":
                 j0, nj = step[1:]
                 nc.sync.dma_start(out=u_sb[:, j0 : j0 + nj, :], in_=u_tiles[:, j0 : j0 + nj, :])
             elif kind == "store":
                 j0, nj, halves = step[1:]
-                cols = slice(halves[0] * HALF, (halves[-1] + 1) * HALF)
-                nc.sync.dma_start(out=out_tiles[:, j0 : j0 + nj, cols], in_=res[:, j0 : j0 + nj, cols])
+                parts = parts_of(j0, halves[0]) if len(halves) == 1 else [slice(0, N)]
+                for cols in parts:
+                    nc.sync.dma_start(out=out_tiles[:, j0 : j0 + nj, cols], in_=res[:, j0 : j0 + nj, cols])
             elif kind == "consts":
                 nc.vector.tensor_copy(out=rate_all[:].rearrange("p (n i) -> p n i", i=N // P), in_=rate_ps[:].rearrange("p i n -> p n i"))
                 nc.vector.tensor_copy(out=keep_cols[:], in_=keep_ps[:, 0:TILES])
@@ -263,14 +289,15 @@ def tile_leaky_iterative_learning_update_e2_kernel(tc, e_words, e_scales, gain, 
                 )
             elif kind == "op1":
                 j, h = step[1:]
-                cols = slice(h * HALF, (h + 1) * HALF)
-                nc.vector.tensor_tensor(out=res[:, j, cols], in0=bank[(j, h)][:], in1=rate_all[:, cols], op=MULT)
+                for cols in parts_of(j, h):
+                    in_bank = slice(cols.start - h * HALF, cols.stop - h * HALF)
+                    nc.vector.tensor_tensor(out=res[:, j, cols], in0=bank[(j, h)][:, in_bank], in1=rate_all[:, cols], op=MULT)
             else:
                 j, h = step[1:]
-                cols = slice(h * HALF, (h + 1) * HALF)
-                nc.vector.scalar_tensor_tensor(
-                    out=res[:, j, cols], in0=u_sb[:, j, cols], scalar=keep_cols[:, j : j + 1], in1=res[:, j, cols], op0=MULT, op1=ADD
-                )
+                for cols in parts_of(j, h):
+                    nc.vector.scalar_tensor_tensor(
+                        out=res[:, j, cols], in0=u_sb[:, j, cols], scalar=keep_cols[:, j : j + 1], in1=res[:, j, cols], op0=MULT, op1=ADD
+                    )
 
         for engine, step in merge(queues):
             emit(engine, step)

@@ -26,7 +26,7 @@ GROUP_BUFS = 6
 RAW_TILES = 9
 FIRST_TILES = 6
 
-def plan_with(w0=6, gs=0, blocks=((6,2),(8,4)), groups=((6,2),(8,1),(9,1),(10,1),(11,1)), uat=(3,8,12,16,20,24), mix=6, lag=2, pre=4, rate=2, vhelp=(), split=((0,2,1),(2,1,1),(3,1,0),(4,2,0)), fill=0, qa=0, seq=1, big=0, usz=2, eup=0, cut=0, n1=6):
+def plan_with(w0=6, gs=0, blocks=((6,2),(8,4)), groups=((6,2),(8,1),(9,1),(10,1),(11,1)), uat=(3,8,12,16,20,24), mix=6, lag=2, pre=4, rate=2, vhelp=(), split=((0,2,1),(2,1,1),(3,1,0),(4,2,0)), fill=0, qa=0, seq=1, big=0, usz=2, eup=0, cut=0, n1=6, sc0=2, sc1=0):
     lead=8-w0
     sync=[]
     tail=[]
@@ -37,6 +37,10 @@ def plan_with(w0=6, gs=0, blocks=((6,2),(8,4)), groups=((6,2),(8,1),(9,1),(10,1)
         else:
             sync.insert(len(sync)-(eup if g==5 else 0),('err',g,(0,)))
             tail.append(('err',g,(1,)))
+    if sc1<0: sync.insert(sc0,('scales',(0,1)))
+    else:
+        sync.insert(len(sync)-sc1,('scales',(1,)))
+        sync.insert(sc0,('scales',(0,)))
     gains=[('gain',g,j,n) for (j,n) in blocks for g in range(6)]
     rest=[]
     while tail:
@@ -102,8 +106,9 @@ def plan_with(w0=6, gs=0, blocks=((6,2),(8,4)), groups=((6,2),(8,1),(9,1),(10,1)
 
 
 def plan():
-    queues = plan_with(**{'gs': 0, 'mix': 6, 'lag': 5, 'pre': 8, 'rate': 2, 'qa': 0, 'seq': 2, 'big': 2, 'n1': 6, 'groups': ((6, 1), (7, 1), (8, 1), (9, 1), (10, 1), (11, 1)), 'split': ((0, 1, 1), (1, 1, 0), (2, 2, 1), (4, 2, 0)), 'w0': 6, 'blocks': ((6,3),(9,3)), 'fill': 6, 'uat': (4,10,13,15,30,30)})
+    queues = plan_with(**{'gs': 0, 'mix': 6, 'lag': 5, 'pre': 8, 'rate': 2, 'qa': 0, 'seq': 2, 'big': 2, 'n1': 6, 'groups': ((6, 1), (7, 1), (8, 1), (9, 1), (10, 1), (11, 1)), 'split': ((0, 1, 1), (1, 1, 0), (2, 2, 1), (4, 2, 0)), 'w0': 6, 'blocks': ((6,3),(9,3)), 'fill': 6, 'uat': (4,10,13,15,30,30),'sc0':2,'sc1':-1})
     queues["dve"].insert(6, ("consts",))
+    queues["pe"].insert(0, ("turn",))
     return queues
 
 
@@ -130,13 +135,15 @@ def needs(step, units):
         return [("inter", step[1], j) for j in range(step[2], step[2] + step[3])]
     if kind == "mm":
         j, h, g = step[1:]
-        keys = [("quant", g, j), ("err", g, h)]
+        keys = [("quant", g, j), ("err", g, h), ("scales", h)]
         place = units.index((j, h))
         if g == 0 and place >= BANKS:
             keys.append(("op1",) + units[place - BANKS])
         if g == 0 and place in (6, 7):
             keys.append(("consts",))
         return keys
+    if kind == "consts":
+        return [("turn",)]
     if kind == "op1":
         return [("mm", step[1], step[2], PASSES - 1), ("consts",)]
     if kind == "op2":
@@ -147,7 +154,7 @@ def needs(step, units):
 
 
 def merge(queues):
-    units = [(s[1], s[2]) for s in queues["pe"] if s[3] == 0]
+    units = [(s[1], s[2]) for s in queues["pe"] if s[0] == "mm" and s[3] == 0]
     made = set()
     place = {engine: 0 for engine in queues}
     waiting = {"act": [], "dve": []}
@@ -204,15 +211,9 @@ def tile_leaky_iterative_learning_update_e2_kernel(tc, e_words, e_scales, gain, 
         nc.vector.memset(keep_rows[:], 0.0)
         nc.scalar.dma_start(out=rate_cols[:], in_=rate.rearrange("(p i) -> p i", p=P))
         nc.scalar.dma_start(out=keep_rows[0:TILES, :], in_=keep.rearrange("(j p) -> j p", p=P))
-        for r in range(4):
-            src = e_scales[:, r:16:4, :].rearrange("g q n -> q g n").bitcast(I32)
-            nc.gpsimd.dma_start(out=err_scales[r:P:32, :, :].bitcast(I32), in_=src)
         make_identity(nc, ident[:])
         rate_ps = psum.tile([P, N // P, P], BF16, tag="bank6", name="rate_ps")
-        for i in range(N // P):
-            nc.tensor.transpose(rate_ps[:, i, :], rate_cols[:, i : i + 1].to_broadcast([P, P]), ident[:])
         keep_ps = psum.tile([P, P], BF16, tag="bank7", name="keep_ps")
-        nc.tensor.transpose(keep_ps[:], keep_rows[:], ident[:])
 
         raw_view = {}
         grouped = {}
@@ -241,6 +242,14 @@ def tile_leaky_iterative_learning_update_e2_kernel(tc, e_words, e_scales, gain, 
                 lo, hi = halves[0] * HALF, (halves[-1] + 1) * HALF
                 src = e_words[g].rearrange("p n t -> p (n t)")[:, lo * PACK : hi * PACK].bitcast(I32)
                 nc.sync.dma_start(out=err_words[:, g, lo:hi].bitcast(I32), in_=src)
+            elif kind == "scales":
+                for q in (0, 2, 1, 3):
+                    src = e_scales[:, 4 * q : 4 * q + 4, :].rearrange("g r n -> r g n").bitcast(I32)
+                    nc.sync.dma_start(out=err_scales[32 * q : 32 * q + 4, :, :].bitcast(I32), in_=src)
+            elif kind == "turn":
+                for i in range(N // P):
+                    nc.tensor.transpose(rate_ps[:, i, :], rate_cols[:, i : i + 1].to_broadcast([P, P]), ident[:])
+                nc.tensor.transpose(keep_ps[:], keep_rows[:], ident[:])
             elif kind == "u":
                 j0, nj = step[1:]
                 nc.sync.dma_start(out=u_sb[:, j0 : j0 + nj, :], in_=u_tiles[:, j0 : j0 + nj, :])

from contextlib import ExitStack

import concourse.mybir as mybir
from concourse.masks import make_identity

K, M, N = 3072, 1536, 1024
FLOPS = 2 * K * M * N

F32 = mybir.dt.float32
BF16 = mybir.dt.bfloat16
I32 = mybir.dt.int32
U32 = mybir.dt.uint32
U8 = mybir.dt.uint8
E4M3X4 = mybir.dt.float8_e4m3fn_x4
E5M2X4 = mybir.dt.float8_e5m2_x4
MULT = mybir.AluOpType.mult
ADD = mybir.AluOpType.add

P = 128
PACK = 4
PASSES = K // (P * PACK)
TILES = M // P
HALF = 512
BANKS = 8
GROUP_BUFS = 6
RAW_TILES = 9
FIRST_TILES = 6

def plan_with(w0=6, gs=0, blocks=((6,2),(8,4)), groups=((6,2),(8,1),(9,1),(10,1),(11,1)), uat=(3,8,12,16,20,24), mix=6, lag=2, pre=4, rate=2, vhelp=(), split=((0,2,1),(2,1,1),(3,1,0),(4,2,0)), fill=0, qa=0, seq=1, big=0, usz=2, eup=0, cut=0, n1=6, sc0=2, sc1=0):
    lead=8-w0
    sync=[]
    tail=[]
    for g in range(6):
        if g>=6-cut: sync+=[('gain',g,0,2),('gain',g,2,w0-2)]
        else: sync.append(('gain',g,0,w0))
        if g<gs: sync.append(('err',g,(0,1)))
        else:
            sync.insert(len(sync)-(eup if g==5 else 0),('err',g,(0,)))
            tail.append(('err',g,(1,)))
    if sc1<0: sync.insert(sc0,('scales',(0,1)))
    else:
        sync.insert(len(sync)-sc1,('scales',(1,)))
        sync.insert(sc0,('scales',(0,)))
    gains=[('gain',g,j,n) for (j,n) in blocks for g in range(6)]
    rest=[]
    while tail:
        rest+=tail[:mix]
        tail=tail[mix:]
        if tail: rest.append(gains.pop(0))
    rest+=gains
    for i in range(len(rest)+1):
        for kk,p in enumerate(uat[:12//usz]):
            if min(p,len(rest))==i: sync.append(('u',usz*kk,usz))
        if i<len(rest): sync.append(rest[i])
    for j in range(0,2*big,2): sync.append(('store',j,2,(0,1)))
    for j in range(2*big,11): sync.append(('store',j,1,(0,1)))
    sync+= [('store',11,1,(0,)),('store',11,1,(1,))]
    act=[]
    dve=[]
    pe=[]
    for g in range(6):
        mine=[(j,n) for (j,n,v) in split if v]
        dve+=[('inter',g,j,n) for (j,n) in mine]
        act+=[('inter',g,j,n) for (j,n,v) in split if not v]
        dve+=[('quant',g,j,n) for (j,n,v) in split]
        pe+=[('mm',j,0,g) for j in range(w0)]
        if g<gs: pe+=[('mm',j,1,g) for j in range(lead)]
    pe+=[('mm',j,1,g) for g in range(gs,6) for j in range(lead)]
    pe+=[('mm',j,1,g) for j in range(lead,w0) for g in range(6)]
    steps=[(j,n,g) for (j,n) in groups for g in range(6)]
    for (j,n,g) in steps: pe+=[('mm',jj,h,g) for jj in range(j,j+n) for h in range(2) if jj<12-seq]
    pe+=[('mm',j,h,g) for j in range(12-seq,12) for h in range(2) for g in range(6)]
    for k in range(fill):
        steps.insert(2*k+1,steps.pop(6+k))
    pend=[('op1',j,0) for j in range(n1 if n1<w0 else w0)]
    for j in range(w0):
        if j>=n1: pend.append(('op1',j,0))
        pend+=[('op1',j,1),('op2',j,0),('op2',j,1)] if j else [('op2',j,0),('op1',j,1),('op2',j,1)]
    for unused in range(pre): dve.append(pend.pop(0))
    later=[]
    credit=0
    for i,(j,n,g) in enumerate(steps):
        if i in vhelp: dve.append(('inter',g,j,n))
        else: act.append(('inter',g,j,n))
        if i in vhelp and pend:
            dve.append(pend.pop(0))
            credit-=1
        dve.append(('quant',g,j,n))
        for (due,ops) in list(later):
            if due<=i:
                pend+=ops
                later.remove((due,ops))
        if i>=qa: credit+=rate*n/2
        while credit>=1 and pend:
            dve.append(pend.pop(0))
            credit-=1
        if not pend: credit=0
        if g==5:
            ops=[]
            for jj in range(j,j+n): ops+=[('op1',jj,0),('op1',jj,1),('op2',jj,0),('op2',jj,1)]
            if j+n==12: ops[-3:]=[ops[-2],ops[-3],ops[-1]]
            later.append((i+lag,ops))
    for due,ops in later: pend+=ops
    dve+=pend
    return dict(sync=sync,act=act,dve=dve,pe=pe)


def plan():
    queues = plan_with(**{'gs': 0, 'mix': 6, 'lag': 5, 'pre': 8, 'rate': 2, 'qa': 0, 'seq': 2, 'big': 2, 'n1': 6, 'groups': ((6, 1), (7, 1), (8, 1), (9, 1), (10, 1), (11, 1)), 'split': ((0, 1, 1), (1, 1, 0), (2, 2, 1), (4, 2, 0)), 'w0': 6, 'blocks': ((6,3),(9,3)), 'fill': 6, 'uat': (4,10,13,15,30,30),'sc0':2,'sc1':-1})
    queues["dve"].insert(6, ("consts",))
    queues["pe"].insert(0, ("turn",))
    return queues


def covers(step):
    kind = step[0]
    if kind in ("gain", "inter", "quant"):
        return [(kind, step[1], j) for j in range(step[2], step[2] + step[3])]
    if kind == "err":
        return [(kind, step[1], h) for h in step[2]]
    if kind == "scales":
        return [(kind, g) for g in step[1]]
    if kind == "u":
        return [(kind, j) for j in range(step[1], step[1] + step[2])]
    return [step]


def needs(step, units):
    kind = step[0]
    if kind == "gain":
        return [("inter", step[1], j) for j in range(FIRST_TILES) if step[2] >= RAW_TILES]
    if kind == "inter":
        return [("gain", step[1], j) for j in range(step[2], step[2] + step[3])]
    if kind == "quant":
        return [("inter", step[1], j) for j in range(step[2], step[2] + step[3])]
    if kind == "mm":
        j, h, g = step[1:]
        keys = [("quant", g, j), ("err", g, h), ("scales", h)]
        place = units.index((j, h))
        if g == 0 and place >= BANKS:
            keys.append(("op1",) + units[place - BANKS])
        if g == 0 and place in (6, 7):
            keys.append(("consts",))
        return keys
    if kind == "consts":
        return [("turn",)]
    if kind == "op1":
        return [("mm", step[1], step[2], PASSES - 1), ("consts",)]
    if kind == "op2":
        return [("op1", step[1], step[2]), ("u", step[1])]
    if kind == "store":
        return [("op2", j, h) for j in range(step[1], step[1] + step[2]) for h in step[3]]
    return []


def merge(queues):
    units = [(s[1], s[2]) for s in queues["pe"] if s[0] == "mm" and s[3] == 0]
    made = set()
    place = {engine: 0 for engine in queues}
    waiting = {"act": [], "dve": []}
    order = []
    total = sum(len(q) for q in queues.values())
    while len(order) < total:
        before = len(order)
        for engine, queue in queues.items():
            if place[engine] == len(queue):
                continue
            step = queue[place[engine]]
            if not all(key in made for key in needs(step, units)):
                continue
            if step[0] == "inter":
                ring = waiting[engine]
                if len(ring) >= GROUP_BUFS and ("quant", ring[-GROUP_BUFS][1], ring[-GROUP_BUFS][2]) not in made:
                    continue
                ring.append(step)
            for key in covers(step):
                made.add(key)
            order.append((engine, step))
            place[engine] += 1
        assert len(order) > before
    return order


def tile_leaky_iterative_learning_update_e2_kernel(tc, e_words, e_scales, gain, u, keep, rate, out):
    nc = tc.nc
    queues = plan()

    with ExitStack() as ctx:
        hold = ctx.enter_context(tc.tile_pool(name="hold", bufs=1))
        stage = ctx.enter_context(tc.tile_pool(name="stage", bufs=GROUP_BUFS))
        psum = ctx.enter_context(tc.psum_pool(name="psum", bufs=1))
        ctx.enter_context(tc.manual_schedule())

        err_words = hold.tile([P, PASSES, N], U32, align_bytes=64)
        err_scales = hold.tile([P, PASSES, N], U8, align_bytes=64)
        gain_words = hold.tile([P, PASSES, M], U32, align_bytes=64)
        gain_scales = hold.tile([P, PASSES, M], U8, align_bytes=64)
        raw = hold.tile([P, PASSES, PACK * RAW_TILES * P], BF16, align_bytes=64)
        u_sb = hold.tile([P, TILES, N], BF16)
        res = hold.tile([P, TILES, N], F32)
        ident = hold.tile([P, P], BF16)
        keep_rows = hold.tile([P, P], BF16)
        rate_cols = hold.tile([P, N // P], BF16)
        keep_cols = hold.tile([P, TILES], F32)
        rate_all = hold.tile([P, N], BF16)

        u_tiles = u.rearrange("(j p) n -> p j n", p=P)
        out_tiles = out.rearrange("(j p) n -> p j n", p=P)

        nc.vector.memset(err_scales[:].bitcast(I32), 0)
        nc.vector.memset(keep_rows[:], 0.0)
        nc.scalar.dma_start(out=rate_cols[:], in_=rate.rearrange("(p i) -> p i", p=P))
        nc.scalar.dma_start(out=keep_rows[0:TILES, :], in_=keep.rearrange("(j p) -> j p", p=P))
        make_identity(nc, ident[:])
        rate_ps = psum.tile([P, N // P, P], BF16, tag="bank6", name="rate_ps")
        keep_ps = psum.tile([P, P], BF16, tag="bank7", name="keep_ps")

        raw_view = {}
        grouped = {}
        bank = {}

        def raw_of(g, j0, nj, load):
            first = (load[2] % RAW_TILES) * P * PACK
            rows = raw[:, g, first : first + load[3] * P * PACK].rearrange("p (t w) -> p t w", t=PACK)
            return rows[:, :, (j0 - load[2]) * P : (j0 - load[2] + nj) * P]

        def parts_of(j, h):
            count = 2 if (j, h) == (TILES - 1, 1) else 1
            width = HALF // count
            return [slice(h * HALF + c * width, h * HALF + (c + 1) * width) for c in range(count)]

        def emit(engine, step):
            kind = step[0]
            if kind == "gain":
                g, j0, nj = step[1:]
                for j in range(j0, j0 + nj):
                    raw_view[(j, g)] = step
                rows = gain[g * P * PACK : (g + 1) * P * PACK, j0 * P : (j0 + nj) * P]
                nc.sync.dma_start(out=raw_of(g, j0, nj, step), in_=rows.rearrange("(p t) w -> p t w", t=PACK))
            elif kind == "err":
                g, halves = step[1:]
                lo, hi = halves[0] * HALF, (halves[-1] + 1) * HALF
                src = e_words[g].rearrange("p n t -> p (n t)")[:, lo * PACK : hi * PACK].bitcast(I32)
                nc.sync.dma_start(out=err_words[:, g, lo:hi].bitcast(I32), in_=src)
            elif kind == "scales":
                for q in (0, 2, 1, 3):
                    src = e_scales[:, 4 * q : 4 * q + 4, :].rearrange("g r n -> r g n").bitcast(I32)
                    nc.sync.dma_start(out=err_scales[32 * q : 32 * q + 4, :, :].bitcast(I32), in_=src)
            elif kind == "turn":
                for i in range(N // P):
                    nc.tensor.transpose(rate_ps[:, i, :], rate_cols[:, i : i + 1].to_broadcast([P, P]), ident[:])
                nc.tensor.transpose(keep_ps[:], keep_rows[:], ident[:])
            elif kind == "u":
                j0, nj = step[1:]
                nc.sync.dma_start(out=u_sb[:, j0 : j0 + nj, :], in_=u_tiles[:, j0 : j0 + nj, :])
            elif kind == "store":
                j0, nj, halves = step[1:]
                parts = parts_of(j0, halves[0]) if len(halves) == 1 else [slice(0, N)]
                for cols in parts:
                    nc.sync.dma_start(out=out_tiles[:, j0 : j0 + nj, cols], in_=res[:, j0 : j0 + nj, cols])
            elif kind == "consts":
                nc.vector.tensor_copy(out=rate_all[:].rearrange("p (n i) -> p n i", i=N // P), in_=rate_ps[:].rearrange("p i n -> p n i"))
                nc.vector.tensor_copy(out=keep_cols[:], in_=keep_ps[:, 0:TILES])
            elif kind == "inter":
                g, j0, nj = step[1:]
                side = stage.tile([P, nj * P, PACK], BF16, align_bytes=64, tag="side_" + engine, name="side")
                grouped[(g, j0)] = side
                src = raw_of(g, j0, nj, raw_view[(j0, g)])
                dst = side[:]
                src = src.rearrange("p t (c i) -> p c t i", i=4)
                dst = dst.rearrange("p (c i) t -> p c t i", i=4)
                if engine == "act":
                    nc.scalar.copy(out=dst, in_=src)
                else:
                    nc.vector.tensor_copy(out=dst, in_=src)
            elif kind == "quant":
                g, j0, nj = step[1:]
                cols = slice(j0 * P, (j0 + nj) * P)
                nc.vector.quantize_mx(
                    out=gain_words[:, g, cols].bitcast(E4M3X4),
                    scales=gain_scales[:, g, cols],
                    in_=grouped[(g, j0)][:].rearrange("p w t -> p (w t)"),
                )
            elif kind == "mm":
                j, h, g = step[1:]
                if g == 0:
                    bank[(j, h)] = psum.tile([P, HALF], F32, tag="bank%d" % (len(bank) % BANKS), name="acc")
                m_cols = slice(j * P, (j + 1) * P)
                n_cols = slice(h * HALF, (h + 1) * HALF)
                nc.tensor.matmul_mx(
                    out=bank[(j, h)][:],
                    lhsT=gain_words[:, g, m_cols].bitcast(E4M3X4),
                    lhsT_scale=gain_scales[:, g, m_cols],
                    rhs=err_words[:, g, n_cols].bitcast(E5M2X4),
                    rhs_scale=err_scales[:, g, n_cols],
                    start=(g == 0),
                    stop=(g == PASSES - 1),
                )
            elif kind == "op1":
                j, h = step[1:]
                for cols in parts_of(j, h):
                    in_bank = slice(cols.start - h * HALF, cols.stop - h * HALF)
                    nc.vector.tensor_tensor(out=res[:, j, cols], in0=bank[(j, h)][:, in_bank], in1=rate_all[:, cols], op=MULT)
            else:
                j, h = step[1:]
                for cols in parts_of(j, h):
                    nc.vector.scalar_tensor_tensor(
                        out=res[:, j, cols], in0=u_sb[:, j, cols], scalar=keep_cols[:, j : j + 1], in1=res[:, j, cols], op0=MULT, op1=ADD
                    )

        for engine, step in merge(queues):
            emit(engine, step)
